import numpy as np
import ml_dtypes


def mxq(x, axis, fmt="e4m3"):
    dtype, down = {"e4m3": (ml_dtypes.float8_e4m3fn, 7), "e5m2": (ml_dtypes.float8_e5m2, 14)}[fmt]
    v = np.moveaxis(np.asarray(x, np.float32).astype(ml_dtypes.bfloat16).astype(np.float64), axis, -1)
    blocks = v.reshape(v.shape[:-1] + (-1, 32))
    amax = np.abs(blocks).max(-1, keepdims=True)
    byte = np.maximum(np.where(amax > 0, np.frexp(amax)[1] - 1 + 127, 0) - down, 1)
    scale = np.exp2(byte - 127.0)
    codes = (blocks / scale).astype(np.float32).astype(dtype).astype(np.float64)
    return np.moveaxis((codes * scale).reshape(v.shape), -1, axis)


WIDE = False


def mx_kscale(k):
    if not WIDE:
        return np.ones(k)
    levels = np.array([10, -10, 5, -5, 0])
    if k % 512:
        return np.exp2(np.random.permutation(np.resize(levels, k // 32))).repeat(32)
    a = np.empty((k // 512, 16))
    for p in range(k // 512):
        a[p, :8] = np.random.permutation(np.resize(levels, 8))
        for g in range(8):
            far = levels[np.abs(levels - a[p, g]) >= 10]
            a[p, g + 8] = far[np.random.randint(len(far))]
    return np.exp2(a.ravel()).repeat(32)


def f64(x):
    return np.asarray(x).astype(np.float64)


def striped(idx):
    return np.tile(np.asarray(idx).reshape(-1, 16).T, (8, 1)).astype(np.uint16)


def unstriped(offs):
    return offs[:16].T.reshape(-1).astype(np.int64)


E2M1 = np.array([0.0, 0.5, 1.0, 1.5, 2.0, 3.0, 4.0, 6.0, -0.0, -0.5, -1.0, -1.5, -2.0, -3.0, -4.0, -6.0])


def pack_weight(w, fmt):
    k, n = w.shape
    w = f64(np.asarray(w, np.float32).astype(ml_dtypes.bfloat16)).reshape(k // 32, 32, n)
    amax = np.abs(w).max(1)
    if fmt == "e4m3":
        byte = np.frexp(amax)[1] - 1 + 127 - 7
    else:
        mant, ex = np.frexp(amax / 6.0)
        byte = np.where(mant > 0.5, ex, ex - 1) + 127
    byte = np.clip(np.where(amax > 0, byte, 1), 1, 254)
    scaled = (w * np.exp2(127.0 - byte)[:, None, :]).reshape(k, n).astype(np.float32)
    by_word = np.ascontiguousarray(scaled.reshape(k // 512, 128, 4, n).transpose(0, 1, 3, 2))
    if fmt == "e4m3":
        words = by_word.astype(ml_dtypes.float8_e4m3fn).view(np.uint8)
    else:
        c = by_word.astype(ml_dtypes.float4_e2m1fn).view(np.uint8) & 0xF
        words = (c[..., 0::2] | (c[..., 1::2] << 4)).reshape(k // 512, 128, 2 * n)
    return np.ascontiguousarray(words), np.ascontiguousarray(byte.astype(np.uint8).reshape(k // 512, 16, n))


def unpack_weight(words, scales, fmt):
    g, _, n = scales.shape
    words = np.ascontiguousarray(words).reshape(g, 128, n, -1)
    if fmt == "e4m3":
        vals = words.view(ml_dtypes.float8_e4m3fn).astype(np.float64)
    else:
        nib = np.empty((g, 128, n, 4), np.uint8)
        nib[..., 0::2] = words & 0xF
        nib[..., 1::2] = words >> 4
        vals = E2M1[nib]
    vals = vals * np.repeat(np.exp2(scales.astype(np.float64) - 127.0), 8, axis=1)[..., None]
    return vals.transpose(0, 1, 3, 2).reshape(g * 512, n)


D, T, I, Q, E, G = 512, 2048, 512, 128, 512, 64


def setup_inputs():
    n = np.random.standard_normal
    idx = np.random.permutation(T)[:I]
    fd = mx_kscale(D)
    fi = mx_kscale(I)
    ti = np.ones(T)
    ti[idx] = fi
    keysp = pack_weight(n((D, T)) / fd[:, None], "e2m1")
    return {
        "query": (n((D, Q)) * 0.8 / np.sqrt(D) * fd[:, None]).astype(np.float32),
        "keys_words": keysp[0],
        "keys_scales": keysp[1],
        "lam": (np.random.uniform(0.3, 0.9, (1, Q))).astype(np.float32),
        "shy": (np.random.uniform(20.0, 60.0, (Q, 1))).astype(np.float32),
        "os": (np.random.uniform(4.0, 16.0, (1, I)) * fi).astype(np.float32),
        "vals": (n((E, T)) / ti).astype(np.float32),
        "target": (n((Q, E))).astype(np.float32),
        "offs": striped(idx),
    }


def reference(query, keys_words, keys_scales, lam, shy, os, vals, target, offs):
    idx = unstriped(offs)
    keysu = unpack_weight(keys_words, keys_scales, "e2m1")
    keysidxg = keysu[:, idx]
    queryq = mxq(f64(query), 0, "e4m3")
    a0 = keysidxg.T @ queryq
    a1p = np.pad(a0, ((0, 0), (1, 0)))[:, :Q]
    s0 = a0 + np.tanh(a1p) * f64(lam)
    s = s0.T
    p = np.exp(s - np.max(s, axis=1, keepdims=True))
    r = p / np.sum(p, axis=1, keepdims=True)
    pg = r.reshape(Q, G, I // G).sum(axis=2)
    k0 = np.exp(pg * f64(shy) * (-1.0))
    kr = np.repeat(k0, I // G, axis=1)
    u0 = r * kr
    w = u0 / np.sum(u0, axis=1, keepdims=True)
    wo1 = w * f64(os)
    wt1 = wo1.T
    vt1 = f64(vals)[:, idx].T
    wt1q = mxq(wt1, 0, "e4m3")
    vt1q = mxq(vt1, 0, "e4m3")
    o = wt1q.T @ vt1q
    rs = f64(target) - o
    k2 = np.sqrt(np.mean(np.square(rs), axis=1, keepdims=True) + 0.5)
    y = rs / k2
    return y

@@ -1,0 +1,200 @@
+from contextlib import ExitStack
+
+import concourse.mybir as mybir
+from concourse.masks import make_identity
+
+D, T, I, Q, E, G = 512, 2048, 512, 128, 512, 64
+FLOPS = 2 * D * I * Q + 2 * I * Q * E
+
+F32 = mybir.dt.float32
+BF16 = mybir.dt.bfloat16
+I32 = mybir.dt.int32
+U32 = mybir.dt.uint32
+U16 = mybir.dt.uint16
+U8 = mybir.dt.uint8
+FP8X4 = mybir.dt.float8_e4m3fn_x4
+FP4X4 = mybir.dt.float4_e2m1fn_x4
+ALU = mybir.AluOpType
+ACT = mybir.ActivationFunctionType
+AX = mybir.AxisListType
+
+P = 128
+PACK = 4
+HALF = I // 2
+RUN = I // G
+LIST_COLS = I // 16
+BLOCKS = E // P
+
+
+def tile_attend_afterprevious_crowdshy_remainder_kernel(tc, query, keys_words, keys_scales, lam, shy, slot_factor, vals, target, offs, out):
+    nc = tc.nc
+    with ExitStack() as ctx:
+        sb = ctx.enter_context(tc.tile_pool(name="sb", bufs=1))
+        ps = ctx.enter_context(tc.psum_pool(name="ps", bufs=1))
+
+        key_bytes = sb.tile([P, T], U8, align_bytes=64)
+        nc.vector.memset(key_bytes[:].bitcast(I32), 0)
+
+        offsets = sb.tile([P, LIST_COLS], U16)
+        q_raw = sb.tile([P, PACK, Q], F32)
+        key_words = sb.tile([P, T], U16, align_bytes=64)
+        nc.sync.dma_start(out=q_raw[:], in_=query.rearrange("(p j) q -> p j q", j=PACK))
+        nc.sync.dma_start(out=key_words[:].bitcast(I32), in_=keys_words[0].bitcast(I32))
+        nc.sync.dma_start(offsets[:], offs)
+        scale_rows = keys_scales[0].rearrange("(a r) t -> r a t", r=4)
+        for r in range(4):
+            nc.sync.dma_start(out=key_bytes[r:P:32, :].bitcast(I32), in_=scale_rows[r].bitcast(I32))
+        os_col = sb.tile([P, PACK], F32)
+        lam_col = sb.tile([P, 1], F32)
+        shy_col = sb.tile([P, 1], F32)
+        v_raw = []
+        for b in range(BLOCKS):
+            v_b = sb.tile([P, T], F32, name="v_raw%d" % b)
+            nc.sync.dma_start(out=v_b[:], in_=vals[b * P:(b + 1) * P, :])
+            v_raw.append(v_b)
+            if b == 0:
+                with nc.allow_non_contiguous_dma(reason="one value a partition"):
+                    nc.sync.dma_start(out=lam_col[:], in_=lam.rearrange("o q -> q o"))
+                nc.sync.dma_start(out=os_col[:], in_=slot_factor.rearrange("o (p t) -> p (o t)", t=PACK))
+                nc.sync.dma_start(out=shy_col[:], in_=shy)
+        tgt = sb.tile([P, E], F32)
+        nc.sync.dma_start(out=tgt[:], in_=target)
+
+        ident = sb.tile([P, P], F32)
+        make_identity(nc, ident[:])
+        q_bf = sb.tile([P, 2, Q, PACK], BF16, align_bytes=64)
+        nc.gpsimd.memset(q_bf[:, 1, 0, :], 0.0)
+        a_turn = sb.tile([P, 2, 4 + Q], F32)
+        nc.gpsimd.memset(a_turn[:, :, 3:4], 0.0)
+
+
+        nc.vector.tensor_copy(out=q_bf[:, 0, :, :], in_=q_raw[:].rearrange("p j q -> p q j"))
+        nc.scalar.activation(out=q_bf[:, 1, 1:Q, :], in_=q_raw[:, :, 0:Q - 1].rearrange("p j q -> p q j"), func=ACT.Copy)
+        q_codes = sb.tile([P, 2 * Q], U32, align_bytes=64)
+        q_scales = sb.tile([P, 2 * Q], U8, align_bytes=64)
+        nc.vector.quantize_mx(out=q_codes[:].bitcast(FP8X4), scales=q_scales[:], in_=q_bf[:].rearrange("p a q j -> p (a q j)"))
+
+        kw_b = sb.tile([P, HALF], U16, align_bytes=64)
+        ks_b = sb.tile([P, HALF], U8, align_bytes=64)
+        kw_a = sb.tile([P, HALF], U16, align_bytes=64)
+        ks_a = sb.tile([P, HALF], U8, align_bytes=64)
+        list_a = offsets[:, 0:LIST_COLS // 2]
+        list_b = offsets[:, LIST_COLS // 2:LIST_COLS]
+        nc.vector.tensor_copy(kw_b[:], key_words[:].indirect(list_b))
+        nc.vector.tensor_copy(ks_b[:], key_bytes[:].indirect(list_b))
+        nc.vector.tensor_copy(kw_a[:], key_words[:].indirect(list_a))
+        nc.vector.tensor_copy(ks_a[:], key_bytes[:].indirect(list_a))
+
+        os_ps = ps.tile([P, PACK, P], F32, tag="os")
+        for t in range(PACK):
+            nc.tensor.transpose(os_ps[:, t, :], os_col[:, t:t + 1].to_broadcast([P, P]), ident[:])
+
+        a_slot = ps.tile([P, 2, Q], F32, tag="turn")
+        for j in range(2):
+            cols = slice(j * P, (j + 1) * P)
+            nc.tensor.matmul_mx(out=a_slot[:, j, :], lhsT=kw_b[:, cols].bitcast(FP4X4), lhsT_scale=ks_b[:, cols],
+                                rhs=q_codes[:, 0:Q].bitcast(FP8X4), rhs_scale=q_scales[:, 0:Q], start=True, stop=True)
+        nc.scalar.copy(out=a_turn[:, :, 4:4 + Q], in_=a_slot[:])
+        prev_b = ps.tile([P, HALF], F32, tag="prev_b")
+        own_b = ps.tile([P, HALF], F32, tag="own_b")
+        for j in range(2):
+            nc.tensor.transpose(prev_b[:, j * P:(j + 1) * P], a_turn[:, j, 3:3 + Q], ident[:])
+        for j in range(2):
+            nc.tensor.transpose(own_b[:, j * P:(j + 1) * P], a_turn[:, j, 4:4 + Q], ident[:])
+        prev_a = ps.tile([P, HALF], F32, tag="prev_a")
+        own_a = ps.tile([P, HALF], F32, tag="own_a")
+        nc.tensor.matmul_mx(out=prev_a[:], lhsT=q_codes[:, Q:2 * Q].bitcast(FP8X4), lhsT_scale=q_scales[:, Q:2 * Q],
+                            rhs=kw_a[:].bitcast(FP4X4), rhs_scale=ks_a[:], start=True, stop=True)
+        nc.tensor.matmul_mx(out=own_a[:], lhsT=q_codes[:, 0:Q].bitcast(FP8X4), lhsT_scale=q_scales[:, 0:Q],
+                            rhs=kw_a[:].bitcast(FP4X4), rhs_scale=ks_a[:], start=True, stop=True)
+
+        th_b = sb.tile([P, HALF], F32)
+        th_a = sb.tile([P, HALF], F32)
+        neg_s = sb.tile([P, I], F32)
+        neg_a = sb.tile([P, HALF], F32)
+        min_b = sb.tile([P, 1], F32)
+        neg_max = sb.tile([P, 1], F32)
+        nc.scalar.activation(out=th_b[:], in_=prev_b[:], func=ACT.Tanh, scale=-1.0)
+        nc.scalar.activation(out=th_a[:], in_=prev_a[:], func=ACT.Tanh, scale=-1.0)
+        nc.vector.scalar_tensor_tensor(out=neg_s[:, HALF:I], in0=th_b[:], scalar=lam_col[:], in1=own_b[:], op0=ALU.mult, op1=ALU.subtract)
+        nc.vector.scalar_tensor_tensor(out=neg_a[:], in0=th_a[:], scalar=lam_col[:], in1=own_a[:], op0=ALU.mult, op1=ALU.subtract)
+        nc.vector.tensor_reduce(out=min_b[:], in_=neg_s[:, HALF:I], axis=AX.X, op=ALU.min)
+        nc.vector.tensor_scalar(out=neg_s[:, 0:HALF], in0=neg_a[:], scalar1=1.0, scalar2=min_b[:], op0=ALU.mult, op1=ALU.min, accum_out=neg_max[:])
+
+        p_un = sb.tile([P, I], F32)
+        z_sum = sb.tile([P, 1], F32)
+        nc.scalar.activation(out=p_un[:], in_=neg_s[:], func=ACT.Exp, scale=-1.0, bias=neg_max[:], accum_out=z_sum[:])
+        z_inv = sb.tile([P, 1], F32)
+        damp_scale = sb.tile([P, 1], F32)
+        run_sum = sb.tile([P, G], F32)
+        nc.vector.reciprocal(out=z_inv[:], in_=z_sum[:])
+        nc.vector.tensor_reduce(out=run_sum[:], in_=p_un[:].rearrange("p (g r) -> p g r", r=RUN), axis=AX.X, op=ALU.add)
+        nc.vector.tensor_scalar(out=damp_scale[:], in0=z_inv[:], scalar1=shy_col[:], scalar2=-1.0, op0=ALU.mult, op1=ALU.mult)
+        damp = sb.tile([P, G], F32)
+        nc.scalar.activation(out=damp[:], in_=run_sum[:], func=ACT.Exp, scale=damp_scale[:])
+        p_os = sb.tile([P, I], F32)
+        nc.vector.tensor_tensor(out=p_os[:].rearrange("p (s t) -> p s t", t=PACK), in0=p_un[:].rearrange("p (s t) -> p s t", t=PACK),
+                                in1=os_ps[:].rearrange("p t s -> p s t"), op=ALU.mult)
+        damped = sb.tile([P, G], F32)
+        den = sb.tile([P, 1], F32)
+        den_inv = sb.tile([P, 1], F32)
+        nc.vector.scalar_tensor_tensor(out=damped[:], in0=run_sum[:], scalar=1.0, in1=damp[:], op0=ALU.mult, op1=ALU.mult, accum_out=den[:])
+        nc.vector.reciprocal(out=den_inv[:], in_=den[:])
+        w_bf = sb.tile([P, I], BF16, align_bytes=64)
+        nc.vector.scalar_tensor_tensor(out=w_bf[:].rearrange("p (g r) -> p g r", r=RUN), in0=p_os[:].rearrange("p (g r) -> p g r", r=RUN),
+                                       scalar=den_inv[:], in1=damp[:].unsqueeze(2).to_broadcast([P, G, RUN]), op0=ALU.mult, op1=ALU.mult)
+
+        def turn_and_quantize(rows_bf, tag, name, copy_on_scalar):
+            words = rows_bf[:].bitcast(F32)
+            turned = ps.tile([P, 2, P], F32, tag=tag, name=name + "_ps")
+            for u in range(2):
+                nc.tensor.transpose(turned[:, u, :], words[:, u:2 * P:2], ident[:])
+            grouped = sb.tile([P, P * PACK], BF16, align_bytes=64, name=name + "_grouped")
+            dst = grouped[:].bitcast(F32).rearrange("p (c u) -> p c u", u=2)
+            src = turned[:].rearrange("p u c -> p c u")
+            if copy_on_scalar:
+                nc.scalar.copy(out=dst, in_=src)
+            else:
+                nc.vector.tensor_copy(out=dst, in_=src)
+            codes = sb.tile([P, P], U32, align_bytes=64, name=name + "_codes")
+            scales = sb.tile([P, P], U8, align_bytes=64, name=name + "_scales")
+            nc.vector.quantize_mx(out=codes[:].bitcast(FP8X4), scales=scales[:], in_=grouped[:])
+            return codes, scales
+
+        w_codes, w_scales = turn_and_quantize(w_bf, "turn", "w", True)
+
+        v_quant = []
+        for b in range(BLOCKS):
+            v_bf = sb.tile([P, I], BF16, align_bytes=64, name="v_bf%d" % b)
+            if b == BLOCKS - 1:
+                nc.vector.tensor_copy(v_bf[:, 0:HALF], v_raw[b][:].indirect(list_a))
+            else:
+                nc.scalar.activation(v_bf[:, 0:HALF], v_raw[b][:].indirect(list_a), ACT.Copy)
+            nc.scalar.activation(v_bf[:, HALF:I], v_raw[b][:].indirect(list_b), ACT.Copy)
+            v_quant.append(turn_and_quantize(v_bf, "v%d" % (b % 2), "v%d" % b, False))
+
+        early = (BLOCKS - 1) * P
+        o_early = ps.tile([P, early], F32, tag="prev_b")
+        o_last = ps.tile([P, P], F32, tag="prev_a")
+        for b in range(BLOCKS):
+            dst = o_last[:] if b == BLOCKS - 1 else o_early[:, b * P:(b + 1) * P]
+            nc.tensor.matmul_mx(out=dst, lhsT=w_codes[:].bitcast(FP8X4), lhsT_scale=w_scales[:],
+                                rhs=v_quant[b][0][:].bitcast(FP8X4), rhs_scale=v_quant[b][1][:], start=True, stop=True)
+
+        rest = sb.tile([P, E], F32)
+        squares = sb.tile([P, E], F32)
+        sq_early = sb.tile([P, 1], F32)
+        sq_bias = sb.tile([P, 1], F32)
+        sq_last = sb.tile([P, 1], F32)
+        norm = sb.tile([P, 1], F32)
+        nc.vector.tensor_tensor(out=rest[:, 0:early], in0=tgt[:, 0:early], in1=o_early[:], op=ALU.subtract)
+        nc.vector.scalar_tensor_tensor(out=squares[:, 0:early], in0=rest[:, 0:early], scalar=1.0 / E, in1=rest[:, 0:early],
+                                       op0=ALU.mult, op1=ALU.mult, accum_out=sq_early[:])
+        nc.vector.tensor_scalar(out=sq_bias[:], in0=sq_early[:], scalar1=0.5, scalar2=None, op0=ALU.add)
+        nc.vector.tensor_tensor(out=rest[:, early:E], in0=tgt[:, early:E], in1=o_last[:], op=ALU.subtract)
+        nc.vector.scalar_tensor_tensor(out=squares[:, early:E], in0=rest[:, early:E], scalar=1.0 / E, in1=rest[:, early:E],
+                                       op0=ALU.mult, op1=ALU.mult, accum_out=sq_last[:])
+        nc.scalar.activation(out=norm[:], in_=sq_last[:], func=ACT.Abs_reciprocal_sqrt, bias=sq_bias[:])
+        result = sb.tile([P, E], F32)
+        nc.vector.tensor_scalar(out=result[:], in0=rest[:], scalar1=norm[:], scalar2=None, op0=ALU.mult)
+        nc.sync.dma_start(out=out, in_=result[:])

@@ -1,7 +1,6 @@
 from contextlib import ExitStack
 
 import concourse.mybir as mybir
-from concourse.masks import make_identity
 
 D, T, I, Q, E, G = 512, 2048, 512, 128, 512, 64
 FLOPS = 2 * D * I * Q + 2 * I * Q * E
@@ -24,177 +23,217 @@ HALF = I // 2
 RUN = I // G
 LIST_COLS = I // 16
 BLOCKS = E // P
+AT_VALUES = 0
+AT_KEY_WORDS = BLOCKS * T * 4
+AT_TARGET = AT_KEY_WORDS + T * 2
+AT_COLUMNS = AT_TARGET + E * 4
+LAID_BYTES = AT_COLUMNS + 128
 
 
 def tile_attend_afterprevious_crowdshy_remainder_kernel(tc, query, keys_words, keys_scales, lam, shy, slot_factor, vals, target, offs, out):
     nc = tc.nc
     with ExitStack() as ctx:
         sb = ctx.enter_context(tc.tile_pool(name="sb", bufs=1))
+        laid = ctx.enter_context(tc.tile_pool(name="laid", bufs=1))
         ps = ctx.enter_context(tc.psum_pool(name="ps", bufs=1))
-
-        key_bytes = sb.tile([P, T], U8, align_bytes=64)
-        nc.vector.memset(key_bytes[:].bitcast(I32), 0)
 
         offsets = sb.tile([P, LIST_COLS], U16)
         q_raw = sb.tile([P, PACK, Q], F32)
-        key_words = sb.tile([P, T], U16, align_bytes=64)
-        nc.sync.dma_start(out=q_raw[:], in_=query.rearrange("(p j) q -> p j q", j=PACK))
-        nc.sync.dma_start(out=key_words[:].bitcast(I32), in_=keys_words[0].bitcast(I32))
+        key_bytes = sb.tile([P, T], U8, align_bytes=64)
+        nc.gpsimd.memset(key_bytes[:].bitcast(I32), 0)
         nc.sync.dma_start(offsets[:], offs)
+        nc.sync.dma_start(out=q_raw[:], in_=query.rearrange("(p j) q -> p j q", j=PACK))
         scale_rows = keys_scales[0].rearrange("(a r) t -> r a t", r=4)
         for r in range(4):
             nc.sync.dma_start(out=key_bytes[r:P:32, :].bitcast(I32), in_=scale_rows[r].bitcast(I32))
-        os_col = sb.tile([P, PACK], F32)
-        lam_col = sb.tile([P, 1], F32)
-        shy_col = sb.tile([P, 1], F32)
-        v_raw = []
-        for b in range(BLOCKS):
-            v_b = sb.tile([P, T], F32, name="v_raw%d" % b)
-            nc.sync.dma_start(out=v_b[:], in_=vals[b * P:(b + 1) * P, :])
-            v_raw.append(v_b)
-            if b == 0:
-                with nc.allow_non_contiguous_dma(reason="one value a partition"):
-                    nc.sync.dma_start(out=lam_col[:], in_=lam.rearrange("o q -> q o"))
-                nc.sync.dma_start(out=os_col[:], in_=slot_factor.rearrange("o (p t) -> p (o t)", t=PACK))
-                nc.sync.dma_start(out=shy_col[:], in_=shy)
-        tgt = sb.tile([P, E], F32)
-        nc.sync.dma_start(out=tgt[:], in_=target)
 
+        zeros = laid.tile([P, LAID_BYTES // 4], F32, offset=0, align_bytes=64)
         ident = sb.tile([P, P], F32)
-        make_identity(nc, ident[:])
+        nc.gpsimd.memset(zeros[:, 0:P], 0.0)
+        nc.gpsimd.affine_select(out=ident[:], in_=zeros[:, 0:P], compare_op=ALU.not_equal, fill=1.0, base=0, pattern=[[-1, P]], channel_multiplier=1)
+
+        key_words = laid.tile([P, T], U16, offset=AT_KEY_WORDS, align_bytes=64)
+        v_raw = [laid.tile([P, T], F32, name="v_raw%d" % b, offset=AT_VALUES + b * T * 4, align_bytes=64) for b in range(BLOCKS)]
+        lam_col = laid.tile([P, 1], F32, offset=AT_COLUMNS)
+        shy_col = laid.tile([P, 1], F32, offset=AT_COLUMNS + 32)
+        os_col = laid.tile([P, PACK], F32, offset=AT_COLUMNS + 64)
+        nc.sync.dma_start(out=key_words[:].bitcast(I32), in_=keys_words[0].bitcast(I32))
+        nc.sync.dma_start(out=v_raw[0][:], in_=vals[0:P, :])
+        nc.sync.dma_start(out=v_raw[1][:], in_=vals[P:2 * P, :])
+        with nc.allow_non_contiguous_dma(reason="one value a partition"):
+            nc.sync.dma_start(out=lam_col[:], in_=lam.rearrange("o q -> q o"))
+        nc.sync.dma_start(out=os_col[:], in_=slot_factor.rearrange("o (p t) -> p (o t)", t=PACK))
+        nc.sync.dma_start(out=v_raw[2][:], in_=vals[2 * P:3 * P, :])
+        nc.sync.dma_start(out=shy_col[:], in_=shy)
+        nc.sync.dma_start(out=v_raw[3][:], in_=vals[3 * P:4 * P, :])
+
         q_bf = sb.tile([P, 2, Q, PACK], BF16, align_bytes=64)
         nc.gpsimd.memset(q_bf[:, 1, 0, :], 0.0)
         a_turn = sb.tile([P, 2, 4 + Q], F32)
         nc.gpsimd.memset(a_turn[:, :, 3:4], 0.0)
 
+        rest = sb.tile([P, 4 + E], F32)
+        nc.gpsimd.memset(rest[:, 3:4], 16.0)
 
         nc.vector.tensor_copy(out=q_bf[:, 0, :, :], in_=q_raw[:].rearrange("p j q -> p q j"))
         nc.scalar.activation(out=q_bf[:, 1, 1:Q, :], in_=q_raw[:, :, 0:Q - 1].rearrange("p j q -> p q j"), func=ACT.Copy)
-        q_codes = sb.tile([P, 2 * Q], U32, align_bytes=64)
-        q_scales = sb.tile([P, 2 * Q], U8, align_bytes=64)
-        nc.vector.quantize_mx(out=q_codes[:].bitcast(FP8X4), scales=q_scales[:], in_=q_bf[:].rearrange("p a q j -> p (a q j)"))
 
         kw_b = sb.tile([P, HALF], U16, align_bytes=64)
-        ks_b = sb.tile([P, HALF], U8, align_bytes=64)
+        ks = sb.tile([P, HALF + P], U8, align_bytes=64)
+        ks_b = ks[:, P:P + HALF]
+        ks_a = ks[:, 0:HALF]
         kw_a = sb.tile([P, HALF], U16, align_bytes=64)
-        ks_a = sb.tile([P, HALF], U8, align_bytes=64)
         list_a = offsets[:, 0:LIST_COLS // 2]
         list_b = offsets[:, LIST_COLS // 2:LIST_COLS]
+        q_codes = sb.tile([P, Q], U32, align_bytes=64)
+        q_scales = sb.tile([P, Q], U8, align_bytes=64)
+        nc.vector.quantize_mx(out=q_codes[:].bitcast(FP8X4), scales=q_scales[:], in_=q_bf[:, 0, :, :].rearrange("p q j -> p (q j)"))
+        nc.vector.tensor_copy(ks_b, key_bytes[:].indirect(list_b))
+        prev_codes = sb.tile([P, Q], U32, align_bytes=64)
+        prev_scales = sb.tile([P, Q], U8, align_bytes=64)
+        nc.vector.quantize_mx(out=prev_codes[:].bitcast(FP8X4), scales=prev_scales[:], in_=q_bf[:, 1, :, :].rearrange("p q j -> p (q j)"))
         nc.vector.tensor_copy(kw_b[:], key_words[:].indirect(list_b))
-        nc.vector.tensor_copy(ks_b[:], key_bytes[:].indirect(list_b))
         nc.vector.tensor_copy(kw_a[:], key_words[:].indirect(list_a))
-        nc.vector.tensor_copy(ks_a[:], key_bytes[:].indirect(list_a))
+        tgt = laid.tile([P, E], F32, offset=AT_KEY_WORDS, align_bytes=64)
+        nc.sync.dma_start(out=tgt[:], in_=target)
 
-        os_ps = ps.tile([P, PACK, P], F32, tag="os")
-        for t in range(PACK):
-            nc.tensor.transpose(os_ps[:, t, :], os_col[:, t:t + 1].to_broadcast([P, P]), ident[:])
+        v0_bf = sb.tile([P, I], BF16, align_bytes=64)
+        shared1 = sb.tile([P, 2 * I + HALF], BF16, align_bytes=64)
+        shared2 = sb.tile([P, I], BF16, align_bytes=64)
+        shared3 = sb.tile([P, I], BF16, align_bytes=64)
+        v_bf = [v0_bf[:], shared1[:, 0:I], shared2[:], shared3[:]]
+
+        def gather_on_vector(b, half):
+            nc.vector.tensor_copy(v_bf[b][:, half * HALF:(half + 1) * HALF], v_raw[b][:].indirect((list_a, list_b)[half]))
+
+        def gather_on_scalar(b, half):
+            nc.scalar.activation(v_bf[b][:, half * HALF:(half + 1) * HALF], v_raw[b][:].indirect((list_a, list_b)[half]), ACT.Copy)
+
+        def turn(rows_bf, bank, name):
+            words = rows_bf.bitcast(F32)
+            turned = ps.tile([P, 2, P], F32, tag=bank, name=name + "_ps")
+            for u in range(2):
+                nc.tensor.transpose(turned[:, u, :], words[:, u:2 * P:2], ident[:])
+            return turned
+
+        def weave(turned, grouped, copy):
+            copy(out=grouped.bitcast(F32).rearrange("p (c u) -> p c u", u=2), in_=turned[:].rearrange("p u c -> p c u"))
+
+        def quantize(grouped, codes, name):
+            scales = sb.tile([P, P], U8, align_bytes=64, name=name + "_scales")
+            nc.vector.quantize_mx(out=codes.bitcast(FP8X4), scales=scales[:], in_=grouped)
+            return codes, scales
 
         a_slot = ps.tile([P, 2, Q], F32, tag="turn")
         for j in range(2):
             cols = slice(j * P, (j + 1) * P)
             nc.tensor.matmul_mx(out=a_slot[:, j, :], lhsT=kw_b[:, cols].bitcast(FP4X4), lhsT_scale=ks_b[:, cols],
-                                rhs=q_codes[:, 0:Q].bitcast(FP8X4), rhs_scale=q_scales[:, 0:Q], start=True, stop=True)
+                                rhs=q_codes[:].bitcast(FP8X4), rhs_scale=q_scales[:], start=True, stop=True)
+        nc.vector.tensor_copy(ks_a, key_bytes[:].indirect(list_a))
         nc.scalar.copy(out=a_turn[:, :, 4:4 + Q], in_=a_slot[:])
         prev_b = ps.tile([P, HALF], F32, tag="prev_b")
-        own_b = ps.tile([P, HALF], F32, tag="own_b")
+        own = ps.tile([P, I], F32, tag="own")
+        prev_a = ps.tile([P, HALF], F32, tag="turn")
         for j in range(2):
             nc.tensor.transpose(prev_b[:, j * P:(j + 1) * P], a_turn[:, j, 3:3 + Q], ident[:])
         for j in range(2):
-            nc.tensor.transpose(own_b[:, j * P:(j + 1) * P], a_turn[:, j, 4:4 + Q], ident[:])
-        prev_a = ps.tile([P, HALF], F32, tag="prev_a")
-        own_a = ps.tile([P, HALF], F32, tag="own_a")
-        nc.tensor.matmul_mx(out=prev_a[:], lhsT=q_codes[:, Q:2 * Q].bitcast(FP8X4), lhsT_scale=q_scales[:, Q:2 * Q],
-                            rhs=kw_a[:].bitcast(FP4X4), rhs_scale=ks_a[:], start=True, stop=True)
-        nc.tensor.matmul_mx(out=own_a[:], lhsT=q_codes[:, 0:Q].bitcast(FP8X4), lhsT_scale=q_scales[:, 0:Q],
-                            rhs=kw_a[:].bitcast(FP4X4), rhs_scale=ks_a[:], start=True, stop=True)
+            nc.tensor.transpose(own[:, HALF + j * P:HALF + (j + 1) * P], a_turn[:, j, 4:4 + Q], ident[:])
+        nc.tensor.matmul_mx(out=prev_a[:], lhsT=prev_codes[:].bitcast(FP8X4), lhsT_scale=prev_scales[:],
+                            rhs=kw_a[:].bitcast(FP4X4), rhs_scale=ks_a, start=True, stop=True)
+        nc.tensor.matmul_mx(out=own[:, 0:HALF], lhsT=q_codes[:].bitcast(FP8X4), lhsT_scale=q_scales[:],
+                            rhs=kw_a[:].bitcast(FP4X4), rhs_scale=ks_a, start=True, stop=True)
 
-        th_b = sb.tile([P, HALF], F32)
-        th_a = sb.tile([P, HALF], F32)
-        neg_s = sb.tile([P, I], F32)
-        neg_a = sb.tile([P, HALF], F32)
+        def dealt(ap):
+            return ap.rearrange("p (s t) -> p t s", t=PACK)
+
+        gather_on_vector(0, 0)
+        gather_on_vector(0, 1)
+        th_b = sb.tile([P, PACK, P // 2], F32)
+        th_a = sb.tile([P, PACK, P // 2], F32)
+        neg_s = sb.tile([P, PACK, P], F32)
+        neg_a = shared1[:, HALF:HALF + I].bitcast(F32).rearrange("p (t s) -> p t s", t=PACK)
         min_b = sb.tile([P, 1], F32)
         neg_max = sb.tile([P, 1], F32)
-        nc.scalar.activation(out=th_b[:], in_=prev_b[:], func=ACT.Tanh, scale=-1.0)
-        nc.scalar.activation(out=th_a[:], in_=prev_a[:], func=ACT.Tanh, scale=-1.0)
-        nc.vector.scalar_tensor_tensor(out=neg_s[:, HALF:I], in0=th_b[:], scalar=lam_col[:], in1=own_b[:], op0=ALU.mult, op1=ALU.subtract)
-        nc.vector.scalar_tensor_tensor(out=neg_a[:], in0=th_a[:], scalar=lam_col[:], in1=own_a[:], op0=ALU.mult, op1=ALU.subtract)
-        nc.vector.tensor_reduce(out=min_b[:], in_=neg_s[:, HALF:I], axis=AX.X, op=ALU.min)
-        nc.vector.tensor_scalar(out=neg_s[:, 0:HALF], in0=neg_a[:], scalar1=1.0, scalar2=min_b[:], op0=ALU.mult, op1=ALU.min, accum_out=neg_max[:])
+        nc.scalar.activation(out=th_b[:], in_=dealt(prev_b[:]), func=ACT.Tanh, scale=-1.0)
+        nc.scalar.activation(out=th_a[:], in_=dealt(prev_a[:]), func=ACT.Tanh, scale=-1.0)
+        nc.vector.scalar_tensor_tensor(out=neg_s[:, :, P // 2:P], in0=th_b[:], scalar=lam_col[:], in1=dealt(own[:, HALF:I]), op0=ALU.mult, op1=ALU.subtract)
+        nc.vector.scalar_tensor_tensor(out=neg_a, in0=th_a[:], scalar=lam_col[:], in1=dealt(own[:, 0:HALF]), op0=ALU.mult, op1=ALU.subtract)
+        nc.vector.tensor_reduce(out=min_b[:], in_=neg_s[:, :, P // 2:P], axis=AX.XY, op=ALU.min)
+        nc.vector.tensor_scalar(out=neg_s[:, :, 0:P // 2], in0=neg_a, scalar1=1.0, scalar2=min_b[:], op0=ALU.mult, op1=ALU.min, accum_out=neg_max[:])
+        gather_on_scalar(1, 0)
+        v0_ps = turn(v_bf[0], "v0", "v0")
+        v0_grouped = sb.tile([P, I], BF16, align_bytes=64)
+        weave(v0_ps, v0_grouped[:], nc.scalar.copy)
+        gather_on_vector(1, 1)
+        v0_codes = sb.tile([P, P], U32, align_bytes=64)
+        v_quant = [quantize(v0_grouped[:], v0_codes[:], "v0")]
 
-        p_un = sb.tile([P, I], F32)
+        p_un = sb.tile([P, PACK, P], F32)
         z_sum = sb.tile([P, 1], F32)
         nc.scalar.activation(out=p_un[:], in_=neg_s[:], func=ACT.Exp, scale=-1.0, bias=neg_max[:], accum_out=z_sum[:])
+        gather_on_scalar(2, 0)
+        p_ps = ps.tile([P, PACK, Q], F32, tag="p")
+        for t in range(PACK):
+            nc.tensor.transpose(p_ps[:, t, :], p_un[:, t, :], ident[:])
+
         z_inv = sb.tile([P, 1], F32)
-        damp_scale = sb.tile([P, 1], F32)
-        run_sum = sb.tile([P, G], F32)
+        damp_scale = sb.tile([P, 1], F32, align_bytes=64, tag="damp_scale")
+        run_sum = shared2[:, HALF:HALF + 2 * G].bitcast(F32)
         nc.vector.reciprocal(out=z_inv[:], in_=z_sum[:])
-        nc.vector.tensor_reduce(out=run_sum[:], in_=p_un[:].rearrange("p (g r) -> p g r", r=RUN), axis=AX.X, op=ALU.add)
+        nc.vector.tensor_reduce(out=run_sum, in_=p_un[:].rearrange("p t (g h) -> p g t h", h=2), axis=AX.XY, op=ALU.add)
         nc.vector.tensor_scalar(out=damp_scale[:], in0=z_inv[:], scalar1=shy_col[:], scalar2=-1.0, op0=ALU.mult, op1=ALU.mult)
-        damp = sb.tile([P, G], F32)
-        nc.scalar.activation(out=damp[:], in_=run_sum[:], func=ACT.Exp, scale=damp_scale[:])
-        p_os = sb.tile([P, I], F32)
-        nc.vector.tensor_tensor(out=p_os[:].rearrange("p (s t) -> p s t", t=PACK), in0=p_un[:].rearrange("p (s t) -> p s t", t=PACK),
-                                in1=os_ps[:].rearrange("p t s -> p s t"), op=ALU.mult)
+        damp = shared3[:, 0:2 * G].bitcast(F32)
+        nc.scalar.activation(out=damp, in_=run_sum, func=ACT.Exp, scale=damp_scale[:])
+        p_os = sb.tile([P, Q, PACK], F32)
+        nc.vector.tensor_tensor(out=p_os[:], in0=p_ps[:].rearrange("p t q -> p q t"), in1=os_col[:].unsqueeze(1).to_broadcast([P, Q, PACK]), op=ALU.mult)
+        v1_ps = turn(v_bf[1], "v1", "v1")
+        v1_grouped = sb.tile([P, I], BF16, align_bytes=64, tag="damp_scale")
+        weave(v1_ps, v1_grouped[:], nc.scalar.copy)
         damped = sb.tile([P, G], F32)
         den = sb.tile([P, 1], F32)
-        den_inv = sb.tile([P, 1], F32)
-        nc.vector.scalar_tensor_tensor(out=damped[:], in0=run_sum[:], scalar=1.0, in1=damp[:], op0=ALU.mult, op1=ALU.mult, accum_out=den[:])
+        den_inv = sb.tile([P, 1], F32, align_bytes=64, tag="den_inv")
+        nc.vector.scalar_tensor_tensor(out=damped[:], in0=run_sum, scalar=1.0, in1=damp, op0=ALU.mult, op1=ALU.mult, accum_out=den[:])
+        gather_on_scalar(2, 1)
         nc.vector.reciprocal(out=den_inv[:], in_=den[:])
-        w_bf = sb.tile([P, I], BF16, align_bytes=64)
-        nc.vector.scalar_tensor_tensor(out=w_bf[:].rearrange("p (g r) -> p g r", r=RUN), in0=p_os[:].rearrange("p (g r) -> p g r", r=RUN),
-                                       scalar=den_inv[:], in1=damp[:].unsqueeze(2).to_broadcast([P, G, RUN]), op0=ALU.mult, op1=ALU.mult)
+        factor = sb.tile([P, G, 2], F32)
+        nc.vector.tensor_scalar(out=factor[:], in0=damp.unsqueeze(2).to_broadcast([P, G, 2]), scalar1=den_inv[:], scalar2=None, op0=ALU.mult)
+        gather_on_scalar(3, 1)
+        gather_on_vector(3, 0)
+        v2_ps = turn(v_bf[2], "v0", "v2")
+        factor_ps = ps.tile([P, Q], F32, tag="turn")
+        nc.tensor.transpose(factor_ps[:], factor[:].rearrange("p g h -> p (g h)"), ident[:])
+        v3_ps = turn(v_bf[3], "own", "v3")
+        w_grouped = laid.tile([P, Q, PACK], BF16, align_bytes=64, offset=AT_VALUES + 3 * T * 4 + 2 * I)
+        nc.vector.tensor_tensor(out=w_grouped[:], in0=p_os[:], in1=factor_ps[:].unsqueeze(2).to_broadcast([P, Q, PACK]), op=ALU.mult)
+        v1_codes = sb.tile([P, P], U32, align_bytes=64, tag="den_inv")
+        v_quant.append(quantize(v1_grouped[:], v1_codes[:], "v1"))
+        v2_grouped = laid.tile([P, I], BF16, align_bytes=64, offset=AT_VALUES + 3 * T * 4)
+        weave(v2_ps, v2_grouped[:], nc.scalar.copy)
+        v3_grouped = sb.tile([P, I], BF16, align_bytes=64)
+        weave(v3_ps, v3_grouped[:], nc.scalar.copy)
+        w_words = sb.tile([P, P], U32, align_bytes=64)
+        w_codes, w_scales = quantize(w_grouped[:].rearrange("p q t -> p (q t)"), w_words[:], "w")
+        v2_codes = sb.tile([P, P], U32, align_bytes=64)
+        v_quant.append(quantize(v2_grouped[:], v2_codes[:], "v2"))
+        v3_codes = sb.tile([P, P], U32, align_bytes=64)
+        v_quant.append(quantize(v3_grouped[:], v3_codes[:], "v3"))
 
-        def turn_and_quantize(rows_bf, tag, name, copy_on_scalar):
-            words = rows_bf[:].bitcast(F32)
-            turned = ps.tile([P, 2, P], F32, tag=tag, name=name + "_ps")
-            for u in range(2):
-                nc.tensor.transpose(turned[:, u, :], words[:, u:2 * P:2], ident[:])
-            grouped = sb.tile([P, P * PACK], BF16, align_bytes=64, name=name + "_grouped")
-            dst = grouped[:].bitcast(F32).rearrange("p (c u) -> p c u", u=2)
-            src = turned[:].rearrange("p u c -> p c u")
-            if copy_on_scalar:
-                nc.scalar.copy(out=dst, in_=src)
-            else:
-                nc.vector.tensor_copy(out=dst, in_=src)
-            codes = sb.tile([P, P], U32, align_bytes=64, name=name + "_codes")
-            scales = sb.tile([P, P], U8, align_bytes=64, name=name + "_scales")
-            nc.vector.quantize_mx(out=codes[:].bitcast(FP8X4), scales=scales[:], in_=grouped[:])
-            return codes, scales
-
-        w_codes, w_scales = turn_and_quantize(w_bf, "turn", "w", True)
-
-        v_quant = []
+        half_e = E // 2
+        o_ps = [ps.tile([P, half_e], F32, tag="prev_b", name="o_lo"), ps.tile([P, half_e], F32, tag="p", name="o_hi")]
         for b in range(BLOCKS):
-            v_bf = sb.tile([P, I], BF16, align_bytes=64, name="v_bf%d" % b)
-            if b == BLOCKS - 1:
-                nc.vector.tensor_copy(v_bf[:, 0:HALF], v_raw[b][:].indirect(list_a))
-            else:
-                nc.scalar.activation(v_bf[:, 0:HALF], v_raw[b][:].indirect(list_a), ACT.Copy)
-            nc.scalar.activation(v_bf[:, HALF:I], v_raw[b][:].indirect(list_b), ACT.Copy)
-            v_quant.append(turn_and_quantize(v_bf, "v%d" % (b % 2), "v%d" % b, False))
+            nc.tensor.matmul_mx(out=o_ps[b // 2][:, (b % 2) * P:(b % 2 + 1) * P], lhsT=w_codes.bitcast(FP8X4), lhsT_scale=w_scales[:],
+                                rhs=v_quant[b][0].bitcast(FP8X4), rhs_scale=v_quant[b][1][:], start=True, stop=True)
 
-        early = (BLOCKS - 1) * P
-        o_early = ps.tile([P, early], F32, tag="prev_b")
-        o_last = ps.tile([P, P], F32, tag="prev_a")
-        for b in range(BLOCKS):
-            dst = o_last[:] if b == BLOCKS - 1 else o_early[:, b * P:(b + 1) * P]
-            nc.tensor.matmul_mx(out=dst, lhsT=w_codes[:].bitcast(FP8X4), lhsT_scale=w_scales[:],
-                                rhs=v_quant[b][0][:].bitcast(FP8X4), rhs_scale=v_quant[b][1][:], start=True, stop=True)
-
-        rest = sb.tile([P, E], F32)
-        squares = sb.tile([P, E], F32)
-        sq_early = sb.tile([P, 1], F32)
-        sq_bias = sb.tile([P, 1], F32)
-        sq_last = sb.tile([P, 1], F32)
+        squares = sb.tile([P, 4 + E], F32)
+        sq_lo = sb.tile([P, 1], F32)
+        sq_hi = sb.tile([P, 1], F32)
         norm = sb.tile([P, 1], F32)
-        nc.vector.tensor_tensor(out=rest[:, 0:early], in0=tgt[:, 0:early], in1=o_early[:], op=ALU.subtract)
-        nc.vector.scalar_tensor_tensor(out=squares[:, 0:early], in0=rest[:, 0:early], scalar=1.0 / E, in1=rest[:, 0:early],
-                                       op0=ALU.mult, op1=ALU.mult, accum_out=sq_early[:])
-        nc.vector.tensor_scalar(out=sq_bias[:], in0=sq_early[:], scalar1=0.5, scalar2=None, op0=ALU.add)
-        nc.vector.tensor_tensor(out=rest[:, early:E], in0=tgt[:, early:E], in1=o_last[:], op=ALU.subtract)
-        nc.vector.scalar_tensor_tensor(out=squares[:, early:E], in0=rest[:, early:E], scalar=1.0 / E, in1=rest[:, early:E],
-                                       op0=ALU.mult, op1=ALU.mult, accum_out=sq_last[:])
-        nc.scalar.activation(out=norm[:], in_=sq_last[:], func=ACT.Abs_reciprocal_sqrt, bias=sq_bias[:])
+        for h in range(2):
+            nc.vector.tensor_tensor(out=rest[:, 4 + h * half_e:4 + (h + 1) * half_e], in0=tgt[:, h * half_e:(h + 1) * half_e], in1=o_ps[h][:], op=ALU.subtract)
+        for cols, acc in ((slice(3, 4 + half_e), sq_lo), (slice(4 + half_e, 4 + E), sq_hi)):
+            nc.vector.scalar_tensor_tensor(out=squares[:, cols], in0=rest[:, cols], scalar=1.0 / E, in1=rest[:, cols],
+                                           op0=ALU.mult, op1=ALU.mult, accum_out=acc[:])
+        nc.scalar.activation(out=norm[:], in_=sq_hi[:], func=ACT.Abs_reciprocal_sqrt, bias=sq_lo[:])
         result = sb.tile([P, E], F32)
-        nc.vector.tensor_scalar(out=result[:], in0=rest[:], scalar1=norm[:], scalar2=None, op0=ALU.mult)
+        nc.vector.tensor_scalar(out=result[:], in0=rest[:, 4:4 + E], scalar1=norm[:], scalar2=None, op0=ALU.mult)
         nc.sync.dma_start(out=out, in_=result[:])

@@ -40,6 +40,8 @@ def tile_attend_afterprevious_crowdshy_remainder_kernel(tc, query, keys_words, k
         offsets = sb.tile([P, LIST_COLS], U16)
         q_raw = sb.tile([P, PACK, Q], F32)
         key_bytes = sb.tile([P, T], U8, align_bytes=64)
+        zeros = laid.tile([P, LAID_BYTES // 4], F32, offset=0, align_bytes=64)
+        nc.gpsimd.memset(zeros[:, 0:P], 0.0)
         nc.gpsimd.memset(key_bytes[:].bitcast(I32), 0)
         nc.sync.dma_start(offsets[:], offs)
         nc.sync.dma_start(out=q_raw[:], in_=query.rearrange("(p j) q -> p j q", j=PACK))
@@ -47,9 +49,7 @@ def tile_attend_afterprevious_crowdshy_remainder_kernel(tc, query, keys_words, k
         for r in range(4):
             nc.sync.dma_start(out=key_bytes[r:P:32, :].bitcast(I32), in_=scale_rows[r].bitcast(I32))
 
-        zeros = laid.tile([P, LAID_BYTES // 4], F32, offset=0, align_bytes=64)
         ident = sb.tile([P, P], F32)
-        nc.gpsimd.memset(zeros[:, 0:P], 0.0)
         nc.gpsimd.affine_select(out=ident[:], in_=zeros[:, 0:P], compare_op=ALU.not_equal, fill=1.0, base=0, pattern=[[-1, P]], channel_multiplier=1)
 
         key_words = laid.tile([P, T], U16, offset=AT_KEY_WORDS, align_bytes=64)
@@ -59,9 +59,9 @@ def tile_attend_afterprevious_crowdshy_remainder_kernel(tc, query, keys_words, k
         os_col = laid.tile([P, PACK], F32, offset=AT_COLUMNS + 64)
         nc.sync.dma_start(out=key_words[:].bitcast(I32), in_=keys_words[0].bitcast(I32))
         nc.sync.dma_start(out=v_raw[0][:], in_=vals[0:P, :])
-        nc.sync.dma_start(out=v_raw[1][:], in_=vals[P:2 * P, :])
         with nc.allow_non_contiguous_dma(reason="one value a partition"):
             nc.sync.dma_start(out=lam_col[:], in_=lam.rearrange("o q -> q o"))
+        nc.sync.dma_start(out=v_raw[1][:], in_=vals[P:2 * P, :])
         nc.sync.dma_start(out=os_col[:], in_=slot_factor.rearrange("o (p t) -> p (o t)", t=PACK))
         nc.sync.dma_start(out=v_raw[2][:], in_=vals[2 * P:3 * P, :])
         nc.sync.dma_start(out=shy_col[:], in_=shy)
@@ -72,13 +72,13 @@ def tile_attend_afterprevious_crowdshy_remainder_kernel(tc, query, keys_words, k
         a_turn = sb.tile([P, 2, 4 + Q], F32)
         nc.gpsimd.memset(a_turn[:, :, 3:4], 0.0)
 
-        rest = sb.tile([P, 4 + E], F32)
-        nc.gpsimd.memset(rest[:, 3:4], 16.0)
+        rest = sb.tile([P, 8 + E], F32)
+        nc.gpsimd.memset(rest[:, 7:8], 16.0)
 
         nc.vector.tensor_copy(out=q_bf[:, 0, :, :], in_=q_raw[:].rearrange("p j q -> p q j"))
         nc.scalar.activation(out=q_bf[:, 1, 1:Q, :], in_=q_raw[:, :, 0:Q - 1].rearrange("p j q -> p q j"), func=ACT.Copy)
 
-        kw_b = sb.tile([P, HALF], U16, align_bytes=64)
+        kw_b = sb.tile([P, HALF], U16, align_bytes=64, tag="words_b")
         ks = sb.tile([P, HALF + P], U8, align_bytes=64)
         ks_b = ks[:, P:P + HALF]
         ks_a = ks[:, 0:HALF]
@@ -89,19 +89,16 @@ def tile_attend_afterprevious_crowdshy_remainder_kernel(tc, query, keys_words, k
         q_scales = sb.tile([P, Q], U8, align_bytes=64)
         nc.vector.quantize_mx(out=q_codes[:].bitcast(FP8X4), scales=q_scales[:], in_=q_bf[:, 0, :, :].rearrange("p q j -> p (q j)"))
         nc.vector.tensor_copy(ks_b, key_bytes[:].indirect(list_b))
-        prev_codes = sb.tile([P, Q], U32, align_bytes=64)
-        prev_scales = sb.tile([P, Q], U8, align_bytes=64)
-        nc.vector.quantize_mx(out=prev_codes[:].bitcast(FP8X4), scales=prev_scales[:], in_=q_bf[:, 1, :, :].rearrange("p q j -> p (q j)"))
         nc.vector.tensor_copy(kw_b[:], key_words[:].indirect(list_b))
         nc.vector.tensor_copy(kw_a[:], key_words[:].indirect(list_a))
         tgt = laid.tile([P, E], F32, offset=AT_KEY_WORDS, align_bytes=64)
         nc.sync.dma_start(out=tgt[:], in_=target)
 
         v0_bf = sb.tile([P, I], BF16, align_bytes=64)
-        shared1 = sb.tile([P, 2 * I + HALF], BF16, align_bytes=64)
+        v1_bf = sb.tile([P, I], BF16, align_bytes=64)
         shared2 = sb.tile([P, I], BF16, align_bytes=64)
         shared3 = sb.tile([P, I], BF16, align_bytes=64)
-        v_bf = [v0_bf[:], shared1[:, 0:I], shared2[:], shared3[:]]
+        v_bf = [v0_bf[:], v1_bf[:], shared2[:], shared3[:]]
 
         def gather_on_vector(b, half):
             nc.vector.tensor_copy(v_bf[b][:, half * HALF:(half + 1) * HALF], v_raw[b][:].indirect((list_a, list_b)[half]))
@@ -130,18 +127,19 @@ def tile_attend_afterprevious_crowdshy_remainder_kernel(tc, query, keys_words, k
             nc.tensor.matmul_mx(out=a_slot[:, j, :], lhsT=kw_b[:, cols].bitcast(FP4X4), lhsT_scale=ks_b[:, cols],
                                 rhs=q_codes[:].bitcast(FP8X4), rhs_scale=q_scales[:], start=True, stop=True)
         nc.vector.tensor_copy(ks_a, key_bytes[:].indirect(list_a))
+        prev_codes = sb.tile([P, Q], U32, align_bytes=64, tag="words_b")
+        prev_scales = sb.tile([P, Q], U8, align_bytes=64)
+        nc.vector.quantize_mx(out=prev_codes[:].bitcast(FP8X4), scales=prev_scales[:], in_=q_bf[:, 1, :, :].rearrange("p q j -> p (q j)"))
         nc.scalar.copy(out=a_turn[:, :, 4:4 + Q], in_=a_slot[:])
         prev_b = ps.tile([P, HALF], F32, tag="prev_b")
-        own = ps.tile([P, I], F32, tag="own")
+        own_b = ps.tile([P, HALF], F32, tag="own")
         prev_a = ps.tile([P, HALF], F32, tag="turn")
         for j in range(2):
             nc.tensor.transpose(prev_b[:, j * P:(j + 1) * P], a_turn[:, j, 3:3 + Q], ident[:])
-        for j in range(2):
-            nc.tensor.transpose(own[:, HALF + j * P:HALF + (j + 1) * P], a_turn[:, j, 4:4 + Q], ident[:])
         nc.tensor.matmul_mx(out=prev_a[:], lhsT=prev_codes[:].bitcast(FP8X4), lhsT_scale=prev_scales[:],
                             rhs=kw_a[:].bitcast(FP4X4), rhs_scale=ks_a, start=True, stop=True)
-        nc.tensor.matmul_mx(out=own[:, 0:HALF], lhsT=q_codes[:].bitcast(FP8X4), lhsT_scale=q_scales[:],
-                            rhs=kw_a[:].bitcast(FP4X4), rhs_scale=ks_a, start=True, stop=True)
+        for j in range(2):
+            nc.tensor.transpose(own_b[:, j * P:(j + 1) * P], a_turn[:, j, 4:4 + Q], ident[:])
 
         def dealt(ap):
             return ap.rearrange("p (s t) -> p t s", t=PACK)
@@ -151,49 +149,54 @@ def tile_attend_afterprevious_crowdshy_remainder_kernel(tc, query, keys_words, k
         th_b = sb.tile([P, PACK, P // 2], F32)
         th_a = sb.tile([P, PACK, P // 2], F32)
         neg_s = sb.tile([P, PACK, P], F32)
-        neg_a = shared1[:, HALF:HALF + I].bitcast(F32).rearrange("p (t s) -> p t s", t=PACK)
+        neg_a_tile = sb.tile([P, PACK, P // 2], F32, align_bytes=64, tag="neg_a")
+        neg_a = neg_a_tile[:]
         min_b = sb.tile([P, 1], F32)
         neg_max = sb.tile([P, 1], F32)
         nc.scalar.activation(out=th_b[:], in_=dealt(prev_b[:]), func=ACT.Tanh, scale=-1.0)
+        own_a = ps.tile([P, HALF], F32, tag="prev_b")
+        nc.tensor.matmul_mx(out=own_a[:], lhsT=q_codes[:].bitcast(FP8X4), lhsT_scale=q_scales[:],
+                            rhs=kw_a[:].bitcast(FP4X4), rhs_scale=ks_a, start=True, stop=True)
         nc.scalar.activation(out=th_a[:], in_=dealt(prev_a[:]), func=ACT.Tanh, scale=-1.0)
-        nc.vector.scalar_tensor_tensor(out=neg_s[:, :, P // 2:P], in0=th_b[:], scalar=lam_col[:], in1=dealt(own[:, HALF:I]), op0=ALU.mult, op1=ALU.subtract)
-        nc.vector.scalar_tensor_tensor(out=neg_a, in0=th_a[:], scalar=lam_col[:], in1=dealt(own[:, 0:HALF]), op0=ALU.mult, op1=ALU.subtract)
+        nc.vector.scalar_tensor_tensor(out=neg_s[:, :, P // 2:P], in0=th_b[:], scalar=lam_col[:], in1=dealt(own_b[:]), op0=ALU.mult, op1=ALU.subtract)
         nc.vector.tensor_reduce(out=min_b[:], in_=neg_s[:, :, P // 2:P], axis=AX.XY, op=ALU.min)
+        nc.vector.scalar_tensor_tensor(out=neg_a, in0=th_a[:], scalar=lam_col[:], in1=dealt(own_a[:]), op0=ALU.mult, op1=ALU.subtract)
         nc.vector.tensor_scalar(out=neg_s[:, :, 0:P // 2], in0=neg_a, scalar1=1.0, scalar2=min_b[:], op0=ALU.mult, op1=ALU.min, accum_out=neg_max[:])
         gather_on_scalar(1, 0)
+        gather_on_scalar(1, 1)
         v0_ps = turn(v_bf[0], "v0", "v0")
-        v0_grouped = sb.tile([P, I], BF16, align_bytes=64)
-        weave(v0_ps, v0_grouped[:], nc.scalar.copy)
-        gather_on_vector(1, 1)
+        v0_grouped = sb.tile([P, I], BF16, align_bytes=64, tag="neg_a")
+        weave(v0_ps, v0_grouped[:], nc.vector.tensor_copy)
         v0_codes = sb.tile([P, P], U32, align_bytes=64)
         v_quant = [quantize(v0_grouped[:], v0_codes[:], "v0")]
 
-        p_un = sb.tile([P, PACK, P], F32)
+        p_un = laid.tile([P, PACK, P], F32, align_bytes=64, offset=AT_VALUES + T * 4)
         z_sum = sb.tile([P, 1], F32)
         nc.scalar.activation(out=p_un[:], in_=neg_s[:], func=ACT.Exp, scale=-1.0, bias=neg_max[:], accum_out=z_sum[:])
+        v1_ps = turn(v_bf[1], "v1", "v1")
+        v1_grouped = sb.tile([P, I], BF16, align_bytes=64)
+        weave(v1_ps, v1_grouped[:], nc.scalar.copy)
         gather_on_scalar(2, 0)
         p_ps = ps.tile([P, PACK, Q], F32, tag="p")
         for t in range(PACK):
             nc.tensor.transpose(p_ps[:, t, :], p_un[:, t, :], ident[:])
 
         z_inv = sb.tile([P, 1], F32)
-        damp_scale = sb.tile([P, 1], F32, align_bytes=64, tag="damp_scale")
-        run_sum = shared2[:, HALF:HALF + 2 * G].bitcast(F32)
+        damp_scale = shared2[:, HALF:HALF + 2].bitcast(F32)
+        run_tile = sb.tile([P, G], F32)
+        run_sum = run_tile[:]
         nc.vector.reciprocal(out=z_inv[:], in_=z_sum[:])
         nc.vector.tensor_reduce(out=run_sum, in_=p_un[:].rearrange("p t (g h) -> p g t h", h=2), axis=AX.XY, op=ALU.add)
-        nc.vector.tensor_scalar(out=damp_scale[:], in0=z_inv[:], scalar1=shy_col[:], scalar2=-1.0, op0=ALU.mult, op1=ALU.mult)
+        nc.vector.tensor_scalar(out=damp_scale, in0=z_inv[:], scalar1=shy_col[:], scalar2=-1.0, op0=ALU.mult, op1=ALU.mult)
         damp = shared3[:, 0:2 * G].bitcast(F32)
-        nc.scalar.activation(out=damp, in_=run_sum, func=ACT.Exp, scale=damp_scale[:])
+        nc.scalar.activation(out=damp, in_=run_sum, func=ACT.Exp, scale=damp_scale)
+        gather_on_scalar(2, 1)
         p_os = sb.tile([P, Q, PACK], F32)
         nc.vector.tensor_tensor(out=p_os[:], in0=p_ps[:].rearrange("p t q -> p q t"), in1=os_col[:].unsqueeze(1).to_broadcast([P, Q, PACK]), op=ALU.mult)
-        v1_ps = turn(v_bf[1], "v1", "v1")
-        v1_grouped = sb.tile([P, I], BF16, align_bytes=64, tag="damp_scale")
-        weave(v1_ps, v1_grouped[:], nc.scalar.copy)
         damped = sb.tile([P, G], F32)
         den = sb.tile([P, 1], F32)
         den_inv = sb.tile([P, 1], F32, align_bytes=64, tag="den_inv")
         nc.vector.scalar_tensor_tensor(out=damped[:], in0=run_sum, scalar=1.0, in1=damp, op0=ALU.mult, op1=ALU.mult, accum_out=den[:])
-        gather_on_scalar(2, 1)
         nc.vector.reciprocal(out=den_inv[:], in_=den[:])
         factor = sb.tile([P, G, 2], F32)
         nc.vector.tensor_scalar(out=factor[:], in0=damp.unsqueeze(2).to_broadcast([P, G, 2]), scalar1=den_inv[:], scalar2=None, op0=ALU.mult)
@@ -224,16 +227,16 @@ def tile_attend_afterprevious_crowdshy_remainder_kernel(tc, query, keys_words, k
             nc.tensor.matmul_mx(out=o_ps[b // 2][:, (b % 2) * P:(b % 2 + 1) * P], lhsT=w_codes.bitcast(FP8X4), lhsT_scale=w_scales[:],
                                 rhs=v_quant[b][0].bitcast(FP8X4), rhs_scale=v_quant[b][1][:], start=True, stop=True)
 
-        squares = sb.tile([P, 4 + E], F32)
+        squares = sb.tile([P, 8 + E], F32)
         sq_lo = sb.tile([P, 1], F32)
         sq_hi = sb.tile([P, 1], F32)
         norm = sb.tile([P, 1], F32)
         for h in range(2):
-            nc.vector.tensor_tensor(out=rest[:, 4 + h * half_e:4 + (h + 1) * half_e], in0=tgt[:, h * half_e:(h + 1) * half_e], in1=o_ps[h][:], op=ALU.subtract)
-        for cols, acc in ((slice(3, 4 + half_e), sq_lo), (slice(4 + half_e, 4 + E), sq_hi)):
+            nc.vector.tensor_tensor(out=rest[:, 8 + h * half_e:8 + (h + 1) * half_e], in0=tgt[:, h * half_e:(h + 1) * half_e], in1=o_ps[h][:], op=ALU.subtract)
+        for cols, acc in ((slice(7, 8 + half_e), sq_lo), (slice(8 + half_e, 8 + E), sq_hi)):
             nc.vector.scalar_tensor_tensor(out=squares[:, cols], in0=rest[:, cols], scalar=1.0 / E, in1=rest[:, cols],
                                            op0=ALU.mult, op1=ALU.mult, accum_out=acc[:])
         nc.scalar.activation(out=norm[:], in_=sq_hi[:], func=ACT.Abs_reciprocal_sqrt, bias=sq_lo[:])
         result = sb.tile([P, E], F32)
-        nc.vector.tensor_scalar(out=result[:], in0=rest[:, 4:4 + E], scalar1=norm[:], scalar2=None, op0=ALU.mult)
+        nc.vector.tensor_scalar(out=result[:], in0=rest[:, 8:8 + E], scalar1=norm[:], scalar2=None, op0=ALU.mult)
         nc.sync.dma_start(out=out, in_=result[:])

@@ -1,6 +1,7 @@
 from contextlib import ExitStack
 
 import concourse.mybir as mybir
+from concourse.masks import make_identity
 
 D, T, I, Q, E, G = 512, 2048, 512, 128, 512, 64
 FLOPS = 2 * D * I * Q + 2 * I * Q * E
@@ -24,9 +25,7 @@ RUN = I // G
 LIST_COLS = I // 16
 BLOCKS = E // P
 AT_VALUES = 0
-AT_KEY_WORDS = BLOCKS * T * 4
-AT_TARGET = AT_KEY_WORDS + T * 2
-AT_COLUMNS = AT_TARGET + E * 4
+AT_COLUMNS = BLOCKS * T * 4
 LAID_BYTES = AT_COLUMNS + 128
 
 
@@ -40,24 +39,29 @@ def tile_attend_afterprevious_crowdshy_remainder_kernel(tc, query, keys_words, k
         offsets = sb.tile([P, LIST_COLS], U16)
         q_raw = sb.tile([P, PACK, Q], F32)
         key_bytes = sb.tile([P, T], U8, align_bytes=64)
-        zeros = laid.tile([P, LAID_BYTES // 4], F32, offset=0, align_bytes=64)
-        nc.gpsimd.memset(zeros[:, 0:P], 0.0)
-        nc.gpsimd.memset(key_bytes[:].bitcast(I32), 0)
+        key_words = sb.tile([P, T], U16, align_bytes=64, tag="key_words")
+        nc.vector.memset(key_bytes[:].bitcast(I32), 0)
         nc.sync.dma_start(offsets[:], offs)
         nc.sync.dma_start(out=q_raw[:], in_=query.rearrange("(p j) q -> p j q", j=PACK))
+        nc.sync.dma_start(out=key_words[:].bitcast(I32), in_=keys_words[0].bitcast(I32))
         scale_rows = keys_scales[0].rearrange("(a r) t -> r a t", r=4)
         for r in range(4):
             nc.sync.dma_start(out=key_bytes[r:P:32, :].bitcast(I32), in_=scale_rows[r].bitcast(I32))
 
         ident = sb.tile([P, P], F32)
-        nc.gpsimd.affine_select(out=ident[:], in_=zeros[:, 0:P], compare_op=ALU.not_equal, fill=1.0, base=0, pattern=[[-1, P]], channel_multiplier=1)
+        make_identity(nc, ident[:])
 
-        key_words = laid.tile([P, T], U16, offset=AT_KEY_WORDS, align_bytes=64)
+        zeros = laid.tile([P, LAID_BYTES // 4], F32, offset=0, align_bytes=64)
+        q_bf = sb.tile([P, 2, Q, PACK], BF16, align_bytes=64, tag="q_bf")
+        a_turn = sb.tile([P, 2, 4 + Q], F32)
+        nc.vector.memset(zeros[:, 0:PACK], 0.0)
+        nc.vector.tensor_copy(out=q_bf[:, 1, 0, :], in_=zeros[:, 0:PACK])
+        nc.vector.tensor_copy(out=a_turn[:, :, 3], in_=zeros[:, 0:2])
+
         v_raw = [laid.tile([P, T], F32, name="v_raw%d" % b, offset=AT_VALUES + b * T * 4, align_bytes=64) for b in range(BLOCKS)]
         lam_col = laid.tile([P, 1], F32, offset=AT_COLUMNS)
         shy_col = laid.tile([P, 1], F32, offset=AT_COLUMNS + 32)
         os_col = laid.tile([P, PACK], F32, offset=AT_COLUMNS + 64)
-        nc.sync.dma_start(out=key_words[:].bitcast(I32), in_=keys_words[0].bitcast(I32))
         nc.sync.dma_start(out=v_raw[0][:], in_=vals[0:P, :])
         with nc.allow_non_contiguous_dma(reason="one value a partition"):
             nc.sync.dma_start(out=lam_col[:], in_=lam.rearrange("o q -> q o"))
@@ -67,38 +71,25 @@ def tile_attend_afterprevious_crowdshy_remainder_kernel(tc, query, keys_words, k
         nc.sync.dma_start(out=shy_col[:], in_=shy)
         nc.sync.dma_start(out=v_raw[3][:], in_=vals[3 * P:4 * P, :])
 
-        q_bf = sb.tile([P, 2, Q, PACK], BF16, align_bytes=64)
-        nc.gpsimd.memset(q_bf[:, 1, 0, :], 0.0)
-        a_turn = sb.tile([P, 2, 4 + Q], F32)
-        nc.gpsimd.memset(a_turn[:, :, 3:4], 0.0)
-
         rest = sb.tile([P, 8 + E], F32)
         nc.gpsimd.memset(rest[:, 7:8], 16.0)
 
         nc.vector.tensor_copy(out=q_bf[:, 0, :, :], in_=q_raw[:].rearrange("p j q -> p q j"))
         nc.scalar.activation(out=q_bf[:, 1, 1:Q, :], in_=q_raw[:, :, 0:Q - 1].rearrange("p j q -> p q j"), func=ACT.Copy)
 
-        kw_b = sb.tile([P, HALF], U16, align_bytes=64, tag="words_b")
-        ks = sb.tile([P, HALF + P], U8, align_bytes=64)
-        ks_b = ks[:, P:P + HALF]
-        ks_a = ks[:, 0:HALF]
-        kw_a = sb.tile([P, HALF], U16, align_bytes=64)
+        kw = sb.tile([P, HALF + P], U16, align_bytes=64)
+        kw_b = kw[:, P:P + HALF]
+        kw_a = kw[:, 0:HALF]
+        ks_b = sb.tile([P, HALF], U8, align_bytes=64, tag="scales_b")
+        ks_a = sb.tile([P, HALF], U8, align_bytes=64)
         list_a = offsets[:, 0:LIST_COLS // 2]
         list_b = offsets[:, LIST_COLS // 2:LIST_COLS]
         q_codes = sb.tile([P, Q], U32, align_bytes=64)
         q_scales = sb.tile([P, Q], U8, align_bytes=64)
         nc.vector.quantize_mx(out=q_codes[:].bitcast(FP8X4), scales=q_scales[:], in_=q_bf[:, 0, :, :].rearrange("p q j -> p (q j)"))
-        nc.vector.tensor_copy(ks_b, key_bytes[:].indirect(list_b))
-        nc.vector.tensor_copy(kw_b[:], key_words[:].indirect(list_b))
-        nc.vector.tensor_copy(kw_a[:], key_words[:].indirect(list_a))
-        tgt = laid.tile([P, E], F32, offset=AT_KEY_WORDS, align_bytes=64)
-        nc.sync.dma_start(out=tgt[:], in_=target)
-
-        v0_bf = sb.tile([P, I], BF16, align_bytes=64)
-        v1_bf = sb.tile([P, I], BF16, align_bytes=64)
-        shared2 = sb.tile([P, I], BF16, align_bytes=64)
-        shared3 = sb.tile([P, I], BF16, align_bytes=64)
-        v_bf = [v0_bf[:], v1_bf[:], shared2[:], shared3[:]]
+        nc.vector.tensor_copy(kw_b, key_words[:].indirect(list_b))
+        nc.vector.tensor_copy(ks_b[:], key_bytes[:].indirect(list_b))
+        nc.vector.tensor_copy(ks_a[:], key_bytes[:].indirect(list_a))
 
         def gather_on_vector(b, half):
             nc.vector.tensor_copy(v_bf[b][:, half * HALF:(half + 1) * HALF], v_raw[b][:].indirect((list_a, list_b)[half]))
@@ -126,9 +117,11 @@ def tile_attend_afterprevious_crowdshy_remainder_kernel(tc, query, keys_words, k
             cols = slice(j * P, (j + 1) * P)
             nc.tensor.matmul_mx(out=a_slot[:, j, :], lhsT=kw_b[:, cols].bitcast(FP4X4), lhsT_scale=ks_b[:, cols],
                                 rhs=q_codes[:].bitcast(FP8X4), rhs_scale=q_scales[:], start=True, stop=True)
-        nc.vector.tensor_copy(ks_a, key_bytes[:].indirect(list_a))
-        prev_codes = sb.tile([P, Q], U32, align_bytes=64, tag="words_b")
-        prev_scales = sb.tile([P, Q], U8, align_bytes=64)
+        nc.vector.tensor_copy(kw_a, key_words[:].indirect(list_a))
+        tgt = sb.tile([P, E], F32, align_bytes=64, tag="key_words")
+        nc.sync.dma_start(out=tgt[:], in_=target)
+        prev_codes = sb.tile([P, Q], U32, align_bytes=64)
+        prev_scales = sb.tile([P, Q], U8, align_bytes=64, tag="scales_b")
         nc.vector.quantize_mx(out=prev_codes[:].bitcast(FP8X4), scales=prev_scales[:], in_=q_bf[:, 1, :, :].rearrange("p q j -> p (q j)"))
         nc.scalar.copy(out=a_turn[:, :, 4:4 + Q], in_=a_slot[:])
         prev_b = ps.tile([P, HALF], F32, tag="prev_b")
@@ -137,9 +130,15 @@ def tile_attend_afterprevious_crowdshy_remainder_kernel(tc, query, keys_words, k
         for j in range(2):
             nc.tensor.transpose(prev_b[:, j * P:(j + 1) * P], a_turn[:, j, 3:3 + Q], ident[:])
         nc.tensor.matmul_mx(out=prev_a[:], lhsT=prev_codes[:].bitcast(FP8X4), lhsT_scale=prev_scales[:],
-                            rhs=kw_a[:].bitcast(FP4X4), rhs_scale=ks_a, start=True, stop=True)
+                            rhs=kw_a.bitcast(FP4X4), rhs_scale=ks_a[:], start=True, stop=True)
         for j in range(2):
             nc.tensor.transpose(own_b[:, j * P:(j + 1) * P], a_turn[:, j, 4:4 + Q], ident[:])
+
+        v0_bf = sb.tile([P, I], BF16, align_bytes=64, tag="q_bf")
+        v1_bf = sb.tile([P, I], BF16, align_bytes=64)
+        shared2 = sb.tile([P, I], BF16, align_bytes=64)
+        shared3 = sb.tile([P, I], BF16, align_bytes=64)
+        v_bf = [v0_bf[:], v1_bf[:], shared2[:], shared3[:]]
 
         def dealt(ap):
             return ap.rearrange("p (s t) -> p t s", t=PACK)
@@ -156,7 +155,7 @@ def tile_attend_afterprevious_crowdshy_remainder_kernel(tc, query, keys_words, k
         nc.scalar.activation(out=th_b[:], in_=dealt(prev_b[:]), func=ACT.Tanh, scale=-1.0)
         own_a = ps.tile([P, HALF], F32, tag="prev_b")
         nc.tensor.matmul_mx(out=own_a[:], lhsT=q_codes[:].bitcast(FP8X4), lhsT_scale=q_scales[:],
-                            rhs=kw_a[:].bitcast(FP4X4), rhs_scale=ks_a, start=True, stop=True)
+                            rhs=kw_a.bitcast(FP4X4), rhs_scale=ks_a[:], start=True, stop=True)
         nc.scalar.activation(out=th_a[:], in_=dealt(prev_a[:]), func=ACT.Tanh, scale=-1.0)
         nc.vector.scalar_tensor_tensor(out=neg_s[:, :, P // 2:P], in0=th_b[:], scalar=lam_col[:], in1=dealt(own_b[:]), op0=ALU.mult, op1=ALU.subtract)
         nc.vector.tensor_reduce(out=min_b[:], in_=neg_s[:, :, P // 2:P], axis=AX.XY, op=ALU.min)

from contextlib import ExitStack

import concourse.mybir as mybir
from concourse.masks import make_identity

D, T, I, Q, E, G = 512, 2048, 512, 128, 512, 64
FLOPS = 2 * D * I * Q + 2 * I * Q * E

F32 = mybir.dt.float32
BF16 = mybir.dt.bfloat16
I32 = mybir.dt.int32
U32 = mybir.dt.uint32
U16 = mybir.dt.uint16
U8 = mybir.dt.uint8
FP8X4 = mybir.dt.float8_e4m3fn_x4
FP4X4 = mybir.dt.float4_e2m1fn_x4
ALU = mybir.AluOpType
ACT = mybir.ActivationFunctionType
AX = mybir.AxisListType

P = 128
PACK = 4
HALF = I // 2
RUN = I // G
LIST_COLS = I // 16
BLOCKS = E // P
AT_VALUES = 0
AT_COLUMNS = BLOCKS * T * 4
LAID_BYTES = AT_COLUMNS + 128


def tile_attend_afterprevious_crowdshy_remainder_kernel(tc, query, keys_words, keys_scales, lam, shy, slot_factor, vals, target, offs, out):
    nc = tc.nc
    with ExitStack() as ctx:
        sb = ctx.enter_context(tc.tile_pool(name="sb", bufs=1))
        laid = ctx.enter_context(tc.tile_pool(name="laid", bufs=1))
        ps = ctx.enter_context(tc.psum_pool(name="ps", bufs=1))

        offsets = sb.tile([P, LIST_COLS], U16)
        q_raw = sb.tile([P, PACK, Q], F32)
        key_bytes = sb.tile([P, T], U8, align_bytes=64)
        key_words = sb.tile([P, T], U16, align_bytes=64, tag="key_words")
        nc.vector.memset(key_bytes[:].bitcast(I32), 0)
        nc.sync.dma_start(offsets[:], offs)
        nc.sync.dma_start(out=q_raw[:], in_=query.rearrange("(p j) q -> p j q", j=PACK))
        nc.sync.dma_start(out=key_words[:].bitcast(I32), in_=keys_words[0].bitcast(I32))
        scale_rows = keys_scales[0].rearrange("(a r) t -> r a t", r=4)
        for r in range(4):
            nc.sync.dma_start(out=key_bytes[r:P:32, :].bitcast(I32), in_=scale_rows[r].bitcast(I32))

        ident = sb.tile([P, P], F32)
        make_identity(nc, ident[:])

        zeros = laid.tile([P, LAID_BYTES // 4], F32, offset=0, align_bytes=64)
        q_bf = sb.tile([P, 2, Q, PACK], BF16, align_bytes=64, tag="q_bf")
        a_turn = sb.tile([P, 2, 4 + Q], F32)
        nc.vector.memset(zeros[:, 0:PACK], 0.0)
        nc.vector.tensor_copy(out=q_bf[:, 1, 0, :], in_=zeros[:, 0:PACK])
        nc.vector.tensor_copy(out=a_turn[:, :, 3], in_=zeros[:, 0:2])

        v_raw = [laid.tile([P, T], F32, name="v_raw%d" % b, offset=AT_VALUES + b * T * 4, align_bytes=64) for b in range(BLOCKS)]
        lam_col = laid.tile([P, 1], F32, offset=AT_COLUMNS)
        shy_col = laid.tile([P, 1], F32, offset=AT_COLUMNS + 32)
        os_col = laid.tile([P, PACK], F32, offset=AT_COLUMNS + 64)
        nc.sync.dma_start(out=v_raw[0][:], in_=vals[0:P, :])
        with nc.allow_non_contiguous_dma(reason="one value a partition"):
            nc.sync.dma_start(out=lam_col[:], in_=lam.rearrange("o q -> q o"))
        nc.sync.dma_start(out=v_raw[1][:], in_=vals[P:2 * P, :])
        nc.sync.dma_start(out=os_col[:], in_=slot_factor.rearrange("o (p t) -> p (o t)", t=PACK))
        nc.sync.dma_start(out=v_raw[2][:], in_=vals[2 * P:3 * P, :])
        nc.sync.dma_start(out=shy_col[:], in_=shy)
        nc.sync.dma_start(out=v_raw[3][:], in_=vals[3 * P:4 * P, :])

        rest = sb.tile([P, 8 + E], F32)
        nc.gpsimd.memset(rest[:, 7:8], 16.0)

        nc.vector.tensor_copy(out=q_bf[:, 0, :, :], in_=q_raw[:].rearrange("p j q -> p q j"))
        nc.scalar.activation(out=q_bf[:, 1, 1:Q, :], in_=q_raw[:, :, 0:Q - 1].rearrange("p j q -> p q j"), func=ACT.Copy)

        kw = sb.tile([P, HALF + P], U16, align_bytes=64)
        kw_b = kw[:, P:P + HALF]
        kw_a = kw[:, 0:HALF]
        ks_b = sb.tile([P, HALF], U8, align_bytes=64, tag="scales_b")
        ks_a = sb.tile([P, HALF], U8, align_bytes=64)
        list_a = offsets[:, 0:LIST_COLS // 2]
        list_b = offsets[:, LIST_COLS // 2:LIST_COLS]
        q_codes = sb.tile([P, Q], U32, align_bytes=64)
        q_scales = sb.tile([P, Q], U8, align_bytes=64)
        nc.vector.quantize_mx(out=q_codes[:].bitcast(FP8X4), scales=q_scales[:], in_=q_bf[:, 0, :, :].rearrange("p q j -> p (q j)"))
        nc.vector.tensor_copy(kw_b, key_words[:].indirect(list_b))
        nc.vector.tensor_copy(ks_b[:], key_bytes[:].indirect(list_b))
        nc.vector.tensor_copy(ks_a[:], key_bytes[:].indirect(list_a))

        def gather_on_vector(b, half):
            nc.vector.tensor_copy(v_bf[b][:, half * HALF:(half + 1) * HALF], v_raw[b][:].indirect((list_a, list_b)[half]))

        def gather_on_scalar(b, half):
            nc.scalar.activation(v_bf[b][:, half * HALF:(half + 1) * HALF], v_raw[b][:].indirect((list_a, list_b)[half]), ACT.Copy)

        def turn(rows_bf, bank, name):
            words = rows_bf.bitcast(F32)
            turned = ps.tile([P, 2, P], F32, tag=bank, name=name + "_ps")
            for u in range(2):
                nc.tensor.transpose(turned[:, u, :], words[:, u:2 * P:2], ident[:])
            return turned

        def weave(turned, grouped, copy):
            copy(out=grouped.bitcast(F32).rearrange("p (c u) -> p c u", u=2), in_=turned[:].rearrange("p u c -> p c u"))

        def quantize(grouped, codes, name):
            scales = sb.tile([P, P], U8, align_bytes=64, name=name + "_scales")
            nc.vector.quantize_mx(out=codes.bitcast(FP8X4), scales=scales[:], in_=grouped)
            return codes, scales

        a_slot = ps.tile([P, 2, Q], F32, tag="turn")
        for j in range(2):
            cols = slice(j * P, (j + 1) * P)
            nc.tensor.matmul_mx(out=a_slot[:, j, :], lhsT=kw_b[:, cols].bitcast(FP4X4), lhsT_scale=ks_b[:, cols],
                                rhs=q_codes[:].bitcast(FP8X4), rhs_scale=q_scales[:], start=True, stop=True)
        nc.vector.tensor_copy(kw_a, key_words[:].indirect(list_a))
        tgt = sb.tile([P, E], F32, align_bytes=64, tag="key_words")
        nc.sync.dma_start(out=tgt[:], in_=target)
        prev_codes = sb.tile([P, Q], U32, align_bytes=64)
        prev_scales = sb.tile([P, Q], U8, align_bytes=64, tag="scales_b")
        nc.vector.quantize_mx(out=prev_codes[:].bitcast(FP8X4), scales=prev_scales[:], in_=q_bf[:, 1, :, :].rearrange("p q j -> p (q j)"))
        nc.scalar.copy(out=a_turn[:, :, 4:4 + Q], in_=a_slot[:])
        prev_b = ps.tile([P, HALF], F32, tag="prev_b")
        own_b = ps.tile([P, HALF], F32, tag="own")
        prev_a = ps.tile([P, HALF], F32, tag="turn")
        for j in range(2):
            nc.tensor.transpose(prev_b[:, j * P:(j + 1) * P], a_turn[:, j, 3:3 + Q], ident[:])
        nc.tensor.matmul_mx(out=prev_a[:], lhsT=prev_codes[:].bitcast(FP8X4), lhsT_scale=prev_scales[:],
                            rhs=kw_a.bitcast(FP4X4), rhs_scale=ks_a[:], start=True, stop=True)
        for j in range(2):
            nc.tensor.transpose(own_b[:, j * P:(j + 1) * P], a_turn[:, j, 4:4 + Q], ident[:])

        v0_bf = sb.tile([P, I], BF16, align_bytes=64, tag="q_bf")
        v1_bf = sb.tile([P, I], BF16, align_bytes=64)
        shared2 = sb.tile([P, I], BF16, align_bytes=64)
        shared3 = sb.tile([P, I], BF16, align_bytes=64)
        v_bf = [v0_bf[:], v1_bf[:], shared2[:], shared3[:]]

        def dealt(ap):
            return ap.rearrange("p (s t) -> p t s", t=PACK)

        gather_on_vector(0, 0)
        gather_on_vector(0, 1)
        th_b = sb.tile([P, PACK, P // 2], F32)
        th_a = sb.tile([P, PACK, P // 2], F32)
        neg_s = sb.tile([P, PACK, P], F32)
        neg_a_tile = sb.tile([P, PACK, P // 2], F32, align_bytes=64, tag="neg_a")
        neg_a = neg_a_tile[:]
        min_b = sb.tile([P, 1], F32)
        neg_max = sb.tile([P, 1], F32)
        nc.scalar.activation(out=th_b[:], in_=dealt(prev_b[:]), func=ACT.Tanh, scale=-1.0)
        own_a = ps.tile([P, HALF], F32, tag="prev_b")
        nc.tensor.matmul_mx(out=own_a[:], lhsT=q_codes[:].bitcast(FP8X4), lhsT_scale=q_scales[:],
                            rhs=kw_a.bitcast(FP4X4), rhs_scale=ks_a[:], start=True, stop=True)
        nc.scalar.activation(out=th_a[:], in_=dealt(prev_a[:]), func=ACT.Tanh, scale=-1.0)
        nc.vector.scalar_tensor_tensor(out=neg_s[:, :, P // 2:P], in0=th_b[:], scalar=lam_col[:], in1=dealt(own_b[:]), op0=ALU.mult, op1=ALU.subtract)
        nc.vector.tensor_reduce(out=min_b[:], in_=neg_s[:, :, P // 2:P], axis=AX.XY, op=ALU.min)
        nc.vector.scalar_tensor_tensor(out=neg_a, in0=th_a[:], scalar=lam_col[:], in1=dealt(own_a[:]), op0=ALU.mult, op1=ALU.subtract)
        nc.vector.tensor_scalar(out=neg_s[:, :, 0:P // 2], in0=neg_a, scalar1=1.0, scalar2=min_b[:], op0=ALU.mult, op1=ALU.min, accum_out=neg_max[:])
        gather_on_scalar(1, 0)
        gather_on_scalar(1, 1)
        v0_ps = turn(v_bf[0], "v0", "v0")
        v0_grouped = sb.tile([P, I], BF16, align_bytes=64, tag="neg_a")
        weave(v0_ps, v0_grouped[:], nc.vector.tensor_copy)
        v0_codes = sb.tile([P, P], U32, align_bytes=64)
        v_quant = [quantize(v0_grouped[:], v0_codes[:], "v0")]

        p_un = laid.tile([P, PACK, P], F32, align_bytes=64, offset=AT_VALUES + T * 4)
        z_sum = sb.tile([P, 1], F32)
        nc.scalar.activation(out=p_un[:], in_=neg_s[:], func=ACT.Exp, scale=-1.0, bias=neg_max[:], accum_out=z_sum[:])
        v1_ps = turn(v_bf[1], "v1", "v1")
        v1_grouped = sb.tile([P, I], BF16, align_bytes=64)
        weave(v1_ps, v1_grouped[:], nc.scalar.copy)
        gather_on_scalar(2, 0)
        p_ps = ps.tile([P, PACK, Q], F32, tag="p")
        for t in range(PACK):
            nc.tensor.transpose(p_ps[:, t, :], p_un[:, t, :], ident[:])

        z_inv = sb.tile([P, 1], F32)
        damp_scale = shared2[:, HALF:HALF + 2].bitcast(F32)
        run_tile = sb.tile([P, G], F32)
        run_sum = run_tile[:]
        nc.vector.reciprocal(out=z_inv[:], in_=z_sum[:])
        nc.vector.tensor_reduce(out=run_sum, in_=p_un[:].rearrange("p t (g h) -> p g t h", h=2), axis=AX.XY, op=ALU.add)
        nc.vector.tensor_scalar(out=damp_scale, in0=z_inv[:], scalar1=shy_col[:], scalar2=-1.0, op0=ALU.mult, op1=ALU.mult)
        damp = shared3[:, 0:2 * G].bitcast(F32)
        nc.scalar.activation(out=damp, in_=run_sum, func=ACT.Exp, scale=damp_scale)
        gather_on_scalar(2, 1)
        p_os = sb.tile([P, Q, PACK], F32)
        nc.vector.tensor_tensor(out=p_os[:], in0=p_ps[:].rearrange("p t q -> p q t"), in1=os_col[:].unsqueeze(1).to_broadcast([P, Q, PACK]), op=ALU.mult)
        damped = sb.tile([P, G], F32)
        den = sb.tile([P, 1], F32)
        den_inv = sb.tile([P, 1], F32, align_bytes=64, tag="den_inv")
        nc.vector.scalar_tensor_tensor(out=damped[:], in0=run_sum, scalar=1.0, in1=damp, op0=ALU.mult, op1=ALU.mult, accum_out=den[:])
        nc.vector.reciprocal(out=den_inv[:], in_=den[:])
        factor = sb.tile([P, G, 2], F32)
        nc.vector.tensor_scalar(out=factor[:], in0=damp.unsqueeze(2).to_broadcast([P, G, 2]), scalar1=den_inv[:], scalar2=None, op0=ALU.mult)
        gather_on_scalar(3, 1)
        gather_on_vector(3, 0)
        v2_ps = turn(v_bf[2], "v0", "v2")
        factor_ps = ps.tile([P, Q], F32, tag="turn")
        nc.tensor.transpose(factor_ps[:], factor[:].rearrange("p g h -> p (g h)"), ident[:])
        v3_ps = turn(v_bf[3], "own", "v3")
        w_grouped = laid.tile([P, Q, PACK], BF16, align_bytes=64, offset=AT_VALUES + 3 * T * 4 + 2 * I)
        nc.vector.tensor_tensor(out=w_grouped[:], in0=p_os[:], in1=factor_ps[:].unsqueeze(2).to_broadcast([P, Q, PACK]), op=ALU.mult)
        v1_codes = sb.tile([P, P], U32, align_bytes=64, tag="den_inv")
        v_quant.append(quantize(v1_grouped[:], v1_codes[:], "v1"))
        v2_grouped = laid.tile([P, I], BF16, align_bytes=64, offset=AT_VALUES + 3 * T * 4)
        weave(v2_ps, v2_grouped[:], nc.scalar.copy)
        v3_grouped = sb.tile([P, I], BF16, align_bytes=64)
        weave(v3_ps, v3_grouped[:], nc.scalar.copy)
        w_words = sb.tile([P, P], U32, align_bytes=64)
        w_codes, w_scales = quantize(w_grouped[:].rearrange("p q t -> p (q t)"), w_words[:], "w")
        v2_codes = sb.tile([P, P], U32, align_bytes=64)
        v_quant.append(quantize(v2_grouped[:], v2_codes[:], "v2"))
        v3_codes = sb.tile([P, P], U32, align_bytes=64)
        v_quant.append(quantize(v3_grouped[:], v3_codes[:], "v3"))

        half_e = E // 2
        o_ps = [ps.tile([P, half_e], F32, tag="prev_b", name="o_lo"), ps.tile([P, half_e], F32, tag="p", name="o_hi")]
        for b in range(BLOCKS):
            nc.tensor.matmul_mx(out=o_ps[b // 2][:, (b % 2) * P:(b % 2 + 1) * P], lhsT=w_codes.bitcast(FP8X4), lhsT_scale=w_scales[:],
                                rhs=v_quant[b][0].bitcast(FP8X4), rhs_scale=v_quant[b][1][:], start=True, stop=True)

        squares = sb.tile([P, 8 + E], F32)
        sq_lo = sb.tile([P, 1], F32)
        sq_hi = sb.tile([P, 1], F32)
        norm = sb.tile([P, 1], F32)
        for h in range(2):
            nc.vector.tensor_tensor(out=rest[:, 8 + h * half_e:8 + (h + 1) * half_e], in0=tgt[:, h * half_e:(h + 1) * half_e], in1=o_ps[h][:], op=ALU.subtract)
        for cols, acc in ((slice(7, 8 + half_e), sq_lo), (slice(8 + half_e, 8 + E), sq_hi)):
            nc.vector.scalar_tensor_tensor(out=squares[:, cols], in0=rest[:, cols], scalar=1.0 / E, in1=rest[:, cols],
                                           op0=ALU.mult, op1=ALU.mult, accum_out=acc[:])
        nc.scalar.activation(out=norm[:], in_=sq_hi[:], func=ACT.Abs_reciprocal_sqrt, bias=sq_lo[:])
        result = sb.tile([P, E], F32)
        nc.vector.tensor_scalar(out=result[:], in0=rest[:, 8:8 + E], scalar1=norm[:], scalar2=None, op0=ALU.mult)
        nc.sync.dma_start(out=out, in_=result[:])
